import numpy as np, ml_dtypes
CORES = [16,17,18,19,150,151]
N = 6
import mx_ref
NC = 128
A = np.float32(0.0125)
BF = ml_dtypes.bfloat16
def cut(t, i, w=512):
    return t[:, w * i:w * i + w]
def tile(rs):
    return np.stack(rs, axis=2).reshape(128, -1).astype(BF)
def setup_inputs(rng):
    def f(*shape):
        return mx_ref.flush((rng.standard_normal(shape, dtype=np.float32) * np.exp2(rng.integers(-2, 3, shape[:-1] + (1,)))).astype(BF))
    return {"q": f(N, 128, 4 * NC), "k": f(N, 128, 4 * 512), "v": f(N, 128, 512)}
def setup_inputs_blocks(rng):
    d = setup_inputs(rng)
    for k in ("v",): d[k] = mx_ref.spread(d[k], rng, 4)
    for k in ("q", "k"): d[k] = mx_ref.spread(d[k], rng, 1)
    return d
def setup_inputs_wide(rng):
    d = setup_inputs(rng)
    for k in ("v",): d[k] = mx_ref.flush((d[k].astype(np.float32) * np.exp2(rng.integers(-8, 9, (N, 1, 1))).astype(np.float32)).astype(BF))
    return d
def setup_inputs_sharp(rng):
    d = setup_inputs(rng); v = d["q"].astype(np.float32).reshape(N, 128, -1, 4)
    d["q"] = mx_ref.flush((v * np.exp2(rng.integers(-2, 4, (N, 1, v.shape[2], 1))).astype(np.float32)).reshape(d["q"].shape).astype(BF))
    return d
def setup_inputs_far(rng):
    d = setup_inputs(rng); d["q"] = (d["q"].astype(np.float32) * 10).astype(BF)
    return d
def setup_inputs_faroff(rng):
    d = setup_inputs(rng); v = d["k"].astype(np.float32).reshape(N, 128, -1, 4)
    d["k"] = mx_ref.flush((v + 192 * rng.standard_normal((1, 128, 1, 4), dtype=np.float32)).reshape(d["k"].shape).astype(BF))
    return d
def reference(q, k, v, own=None):
    ONE = mx_ref.quantize(np.ones((128, 512), BF))
    K = [[mx_ref.quantize(cut(k[j], b)) for b in range(4)] for j in range(N)]; V = [mx_ref.quantize(v[j]) for j in range(N)]
    Q = [mx_ref.quantize(q[i]) for i in range(N)]
    lo = np.zeros((N, N, NC), np.float32); w = lo.copy(); wlo = lo.copy(); whi = lo.copy(); p = np.zeros((N, N, 128, 4 * NC), BF); o = np.zeros((N, 128, NC), np.float32)
    S = [[[mx_ref.matmul(K[j][b], Q[i]) * A for b in range(4)] for i in range(N)] for j in range(N)]
    for j in range(N):
        lo[j] = [np.max(s, axis=(0, 1)) for s in S[j]]
    hi = np.broadcast_to(lo.max(axis=0) + 8, lo.shape).copy()
    c = lo if own is None else own["c"]
    for j in range(N):
        for i in range(N):
            p[j][i] = tile([np.exp(np.maximum(s - c[j][i], -20).astype(np.float64)).astype(np.float32) for s in S[j][i]])
    use = p if own is None else own["p"]
    for i in range(N):
        e = np.exp((c[:, i] - c[:, i].max(axis=0)).astype(np.float64)); wlo[i] = e * (1 - 4e-5); whi[i] = e * (1 + 4e-5)
        w[i] = e if own is None else own["w"][i]
        num = den = 0
        for j in range(N):
            P = mx_ref.quantize(use[j][i])
            num = num + w[i][j].astype(np.float64) * mx_ref.matmul(V[j], P); den = den + w[i][j].astype(np.float64) * mx_ref.matmul(ONE, P)
        o[i] = (num / den).astype(np.float32)
    return {"c": c, "c__lo": lo, "c__hi": hi, "p": p, "w": w, "w__lo": wlo, "w__hi": whi, "o": o}

import numpy as np
from concourse.bass import DstId, RemoteDMATransfer
from concourse.mybir import dt, AluOpType, AxisListType, ActivationFunctionType

N = 6
A = float(np.float32(0.0125))
NG = 4
W1 = 136
F8 = "float8_e4m3fn_x4"
NEG = -1e29

SCRATCH = {
    "qb": ("sbuf", [128, 512], "bfloat16"),
    "kb": ("sbuf", [128, 2048], "bfloat16"),
    "vb": ("sbuf", [128, 512], "bfloat16"),
    "ob1": ("sbuf", [128, 512], "bfloat16"),
    "Qc": ("sbuf", [128, 768], F8), "Qp": ("sbuf", [128, 768], "uint8"),
    "Kc": ("sbuf", [128, 512], F8), "Kp": ("sbuf", [128, 512], "uint8"),
    "Vc": ("sbuf", [128, 128], F8), "Vp": ("sbuf", [128, 128], "uint8"),
    "Oc": ("sbuf", [128, 128], F8), "Op": ("sbuf", [128, 128], "uint8"),
    "rst": ("sbuf", [128, 768], "float32"),
    "m20": ("sbuf", [128, 8], "bfloat16"), "flo": ("sbuf", [128, 8], "bfloat16"),
    "ps": ("psum", [128, 4096], "float32"),
    "crow": ("sbuf", [128, 768], "float32"),
    "la": ("sbuf", [128, N * W1], "float32"),
    "negm": ("sbuf", [128, 4], "float32"),
    "wx": ("sbuf", [128, 768], "float32"), "ws": ("sbuf", [128, 768], "float32"), "wt": ("sbuf", [128, 768], "float32"),
    "acc": ("sbuf", [128, 128], "float32"), "tmp": ("sbuf", [128, 768], "float32"),
    "wl": ("sbuf", [128, 24], "float32"), "den": ("sbuf", [128, 4], "float32"),
    "rx": ("sbuf", [128, 128], "float32"), "rs": ("sbuf", [128, 128], "float32"), "rd": ("sbuf", [128, 128], "float32"),
    "fl": ("sbuf", [128, 128], "float32"), "osb": ("sbuf", [128, 128], "float32"),
}
for _n in ("m", "t", "s", "e", "C", "lt"):
    SCRATCH[_n] = ("sbuf", [128, 256 * NG], "float32")
SCRATCH["u"] = ("sbuf", [128, 8 * NG], "float32")
SCRATCH["x"] = ("sbuf", [128, 1024 * NG], "float32")
SCRATCH["pt"] = ("sbuf", [128, 1024 * NG], "bfloat16")
SCRATCH["pc"] = ("sbuf", [128, 256 * NG], F8)
SCRATCH["pp"] = ("sbuf", [128, 256 * NG], "uint8")
SCRATCH["out"] = ("sbuf", [128, 2 * W1 * NG], "float32")

SEMAPHORES = ["ldq", "ldv", "st", "ms", "mo", "fl", "zq", "zv", "zo", "qdc", "qdp", "qr", "sent", "go", "hm", "hx", "hv", "hr", "ha"]
SEMAPHORES += ["ldk%d" % b for b in range(4)] + ["zk%d" % b for b in range(4)]
for _g in range(NG):
    SEMAPHORES += ["%s%d" % (n, _g) for n in ("ql", "ch", "vq", "lt", "cp", "ex", "cc", "cr", "ae", "pL", "pA")]
    SEMAPHORES += ["%s%d_%d" % (n, _g, b) for n in ("sub", "pS") for b in range(4)]
for _j in range(N):
    SEMAPHORES += ["%s%d" % (n, _j) for n in ("am", "cm", "lm")]


def engines(mask):
    return [e for e in range(mask.bit_length()) if mask >> e & 1]


def to_mask(es):
    return sum(1 << e for e in es)


def rank_program(g, core, T, topo):
    me = T.rank_of(core)
    if me is None:
        return
    CO = T.cores
    sem = T.sem
    V, S, P, Y = g.vector, g.scalar, g.tensor, g.sync
    MAX, ADD, SUB, MUL = AluOpType.max, AluOpType.add, AluOpType.subtract, AluOpType.mult
    Act = ActivationFunctionType

    def place(r):
        return (topo.host(CO[r]), topo.chip(CO[r]))

    def team(r):
        return [s for s in range(N) if place(s) == place(r)]

    def others(r):
        return [s for s in range(N) if place(s) != place(r)]

    def near(a, b):
        return place(a) == place(b)

    def groups(r):
        t, o = team(r), others(r)
        k = t.index(r)
        if len(t) == 4:
            last = t[k ^ 1]
            return [[r], [s for s in t if s not in (r, last)], o, [last]]
        return [[r], [t[1 - k]], o[2 * k:2 * k + 2], o[2 - 2 * k:4 - 2 * k]]

    def early(r, gi):
        return gi == 1 or (gi == 2 and len(team(r)) == 2)

    def slot(r, s):
        return [a for gr in groups(r) for a in gr].index(s)

    def group_of(r, s):
        return [s in gr for gr in groups(r)].index(True)

    def gate(r):
        t, o = team(r), others(r)
        k = t.index(r)
        return o[k // 2] if len(t) == 4 else o[2 * k]

    def split(src, members):
        out = []
        for i, d in enumerate(members):
            es = engines(topo.mask(CO[src], CO[d]))
            w = len(es) // len(members)
            out.append(es[i * w:(i + 1) * w])
        return out

    def dst(d):
        rid, pid = topo.addr(CO[d], core)
        return DstId(rid=rid, pnc=pid)

    G = groups(me)
    nn = [128 * len(x) for x in G]
    base = [sum(nn[:i]) for i in range(NG)]
    mates = [s for s in team(me) if s != me]
    far = gate(me)
    four = len(team(me)) == 4
    fe = engines(topo.mask(core, CO[far]))
    ne = [e for e in engines(topo.mask(core, CO[mates[0]])) if e not in fe]
    inter = [False, False, four, False]

    def ps(gi, b, n):
        c0 = 512 * (4 * (gi % 2) + b)
        return T.ps[:, c0:c0 + n]

    def col(name, gi, a, b, step=1):
        w = 1024 if name in ("x", "pt") else 256
        return T[name][:, w * gi + a:w * gi + b:step]

    Y.dma_start(T.qb[:], T.q[:]).then_inc(sem.ldq, 16)
    for b in range(4):
        Y.dma_start(T.kb[:, 512 * b:512 * b + 512], T.k[:, 512 * b:512 * b + 512]).then_inc(sem["ldk%d" % b], 16)
    S.dma_start(T.vb[:], T.v[:]).then_inc(sem.ldv, 16)

    V.memset(T.m20[:, 0:1], -20.0).then_inc(sem.mo, 1)
    V.memset(T.ob1[:], 1.0).then_inc(sem.mo, 1)
    V.memset(T.rst[:], 0.0).then_inc(sem.mo, 1)
    V.memset(T.wx[:], 0.0).then_inc(sem.ms, 1)
    V.memset(T.rx[:], 0.0).then_inc(sem.ms, 1)
    V.wait_ge(sem.mo, 3)
    V.memset(T.rst[:, 0:768:32], NEG).then_inc(sem.ms, 1)
    V.quantize_mx(T.Oc[:], T.Op[:], T.ob1[:]).then_inc(sem.zo, 1)
    V.wait_ge(sem.ldq, 16)
    V.quantize_mx(T.Qc[:, 0:128], T.Qp[:, 0:128], T.qb[:]).then_inc(sem.zq, 1)
    for b in range(4):
        V.wait_ge(sem["ldk%d" % b], 16)
        c0 = 128 * b
        V.quantize_mx(T.Kc[:, c0:c0 + 128], T.Kp[:, c0:c0 + 128], T.kb[:, 4 * c0:4 * c0 + 512]).then_inc(sem["zk%d" % b], 1)
    S.wait_ge(sem.mo, 3)
    S.activation(T.flo[:, 0:1], T.m20[:, 0:1], Act.Exp).then_inc(sem.fl, 1)

    sent = [0]

    def fused(tr):
        g.remote_dma_fused(tr, local_sem=sem.sent)

    def codes(r):
        return T.Qc[:, 128 * r:128 * r + 128].bitcast(dt.uint8)

    def plane(r):
        return T.Qp[:, 128 * r:128 * r + 128]

    g.wait_ge(sem.zq, 1)
    for view, fs in ((codes, sem.qdc), (plane, sem.qdp)):
        tr = [RemoteDMATransfer(dst_ids=[dst(far)], dma_engine_mask=to_mask(fe), remote_sem=fs, src=view(0), dst=view(slot(far, me)))]
        by = {}
        for d in mates:
            by.setdefault(group_of(d, me), []).append(d)
        ks = sorted(by)
        w = len(ne) // len(ks)
        for i, k in enumerate(ks):
            tr.append(RemoteDMATransfer(dst_ids=[dst(d) for d in by[k]], dma_engine_mask=to_mask(ne[i * w:(i + 1) * w]),
                                        remote_sem=sem["ql%d" % k], srcs=[view(0)], dsts=[view(slot(d, me)) for d in by[k]]))
        fused(tr)
        sent[0] += len(fe) + w * len(ks)

    def local_engines(src, d):
        f = engines(topo.mask(CO[src], CO[gate(src)]))
        n = [e for e in engines(topo.mask(CO[src], CO[d])) if e not in f]
        return len(n) // len(set(group_of(x, src) for x in team(src) if x != src))

    need = [[] for _ in range(NG)]
    for gi in (1, 2, 3):
        c = sum(2 * local_engines(s, me) for s in G[gi] if near(s, me))
        if c:
            need[gi].append((sem["ql%d" % gi], c))
    direct = [s for s in others(me) if gate(s) == me]
    relayed = [s for s in others(me) if gate(s) != me]
    if direct:
        c = sum(len(engines(topo.mask(CO[s], core))) for s in direct)
        gi = group_of(me, direct[0])
        need[gi] += [(sem.qdc, c), (sem.qdp, c)]
        lo = min(slot(me, s) for s in direct)
        first = [s for s in direct if slot(me, s) == lo][0]
        k = len(direct)
        es = engines(topo.mask(core, CO[mates[0]]))
        for isc, fs in ((True, sem.qdc), (False, sem.qdp)):
            def piece(a):
                v = (T.Qc if isc else T.Qp)[:, 128 * a:128 * (a + k)]
                return v.bitcast(dt.uint8) if isc else v
            g.wait_ge(fs, c)
            fused([RemoteDMATransfer(dst_ids=[dst(d) for d in mates], dma_engine_mask=to_mask(es), remote_sem=sem.qr,
                                     srcs=[piece(lo)], dsts=[piece(slot(d, first)) for d in mates])])
            sent[0] += len(es)
    if relayed:
        c = 2 * sum(len(engines(topo.mask(CO[s], core))) for s in sorted(set(gate(x) for x in relayed)))
        need[group_of(me, relayed[0])].append((sem.qr, c))

    def message(gi, k):
        d = G[gi][k]
        if d == me:
            return T.la, me * W1
        return T.out, (2 * gi + k) * W1

    def scores(gi):
        n = nn[gi]
        if gi == 0:
            P.wait_ge(sem.zq, 1)
        for s, c in need[gi]:
            P.wait_ge(s, c)
        for b in range(4):
            if gi == 0:
                P.wait_ge(sem["zk%d" % b], 1)
            if gi >= 2:
                P.wait_ge(sem["sub%d_%d" % (gi - 2, b)], 1)
                if b == 2:
                    P.wait_ge(sem["ae%d" % (gi - 2)], len(G[gi - 2]))
                if b == 3:
                    P.wait_ge(sem["lt%d" % (gi - 2)], 1 + len(G[gi - 2]))
            P.matmul_mx(ps(gi, b, n), T.Kc[:, 128 * b:128 * b + 128], T.Kp[:, 128 * b:128 * b + 128],
                        T.Qc[:, base[gi]:base[gi] + n], T.Qp[:, base[gi]:base[gi] + n], True, True).then_inc(sem["pS%d_%d" % (gi, b)], 1)

    def products(gi):
        n = nn[gi]
        P.wait_ge(sem.zo, 1)
        P.wait_ge(sem.zv, 1)
        P.wait_ge(sem["vq%d" % gi], 2)
        pc, pp = col("pc", gi, 0, n), col("pp", gi, 0, n)
        P.matmul_mx(ps(gi, 3, n), T.Oc[:], T.Op[:], pc, pp, True, True).then_inc(sem["pL%d" % gi], 1)
        P.matmul_mx(ps(gi, 2, n), T.Vc[:], T.Vp[:], pc, pp, True, True).then_inc(sem["pA%d" % gi], 1)

    def first_copy(gi):
        n = nn[gi]
        S.wait_ge(sem["pS%d_0" % gi], 1)
        S.activation(col("m", gi, 0, n), ps(gi, 0, n), Act.Copy).then_inc(sem["cp%d" % gi], 1)

    def maxima(gi):
        n = nn[gi]
        ch, m = sem["ch%d" % gi], col("m", gi, 0, n)
        V.wait_ge(sem["cp%d" % gi], 1)
        for b in (1, 2, 3):
            V.wait_ge(sem["pS%d_%d" % (gi, b)], 1)
            if b > 1:
                V.wait_ge(ch, b - 1)
            V.tensor_tensor(m, ps(gi, b, n), m, MAX).then_inc(ch, 1)

    def fold(gi):
        n = nn[gi]
        ch = sem["ch%d" % gi]
        if gi == 0:
            V.wait_ge(sem.ms, 3)
        V.wait_ge(ch, 3)
        V.transpose(col("t", gi, 0, n), col("m", gi, 0, n)).then_inc(ch, 1)
        V.wait_ge(ch, 4)
        V.tensor_tensor_scan(col("s", gi, 0, n), T.rst[:, 0:n], col("t", gi, 0, n), 0.0, ADD, MAX).then_inc(ch, 1)

    def spread(gi):
        n = nn[gi]
        nb = n // 32
        ch, t, s, u, o, h = sem["ch%d" % gi], T.t, T.s, T.u, 256 * gi, 8 * gi
        z = o + n
        V.wait_ge(ch, 5)
        V.tensor_tensor(u[0:64, h:h + nb], s[0:64, o + 31:z:32], s[64:128, o + 31:z:32], MAX).then_inc(ch, 1)
        V.wait_ge(ch, 6)
        V.tensor_tensor(t[0:32, o:z:32], u[0:32, h:h + nb], u[32:64, h:h + nb], MAX).then_inc(ch, 1)
        V.tensor_tensor(t[32:64, o:z:32], u[0:32, h:h + nb], u[32:64, h:h + nb], MAX).then_inc(ch, 1)
        V.wait_ge(ch, 8)
        V.tensor_copy(t[64:128, o:z:32], t[0:64, o:z:32]).then_inc(ch, 1)
        V.wait_ge(ch, 9)
        V.tensor_tensor_scan(col("e", gi, 0, n), T.rst[:, 0:n], t[:, o:z], 0.0, ADD, MAX).then_inc(ch, 1)
        V.wait_ge(ch, 10)
        V.transpose(col("C", gi, 0, n), col("e", gi, 0, n)).then_inc(ch, 1)
        V.wait_ge(ch, 11)

    def shifts_out(gi):
        S.wait_ge(sem["ch%d" % gi], 9)
        for k, d in enumerate(G[gi]):
            buf, o = message(gi, k)
            S.activation(buf[:, o + 132:o + 136], col("t", gi, 128 * k, 128 * k + 128, 32), Act.Copy, scale=A).then_inc(sem["cc%d" % gi], 1)

    def shift_rows(gi):
        S.wait_ge(sem["ch%d" % gi], 11)
        for k, d in enumerate(G[gi]):
            S.activation(T.crow[0:1, 128 * d:128 * d + 128], T.C[0:1, 256 * gi + 128 * k:256 * gi + 128 * k + 128], Act.Copy, scale=A).then_inc(sem["cr%d" % gi], 1)

    def subtract(gi):
        n = nn[gi]
        for b in range(4):
            V.tensor_tensor(col("x", gi, n * b, n * b + n), ps(gi, b, n), col("C", gi, 0, n), SUB).then_inc(sem["sub%d_%d" % (gi, b)], 1)

    def exps(gi):
        n = nn[gi]
        for b in range(4):
            S.wait_ge(sem["sub%d_%d" % (gi, b)], 1)
            S.activation(col("pt", gi, b, 4 * n, 4), col("x", gi, n * b, n * b + n), Act.Exp, scale=A).then_inc(sem["ex%d" % gi], 1)

    def pack(gi):
        n = nn[gi]
        p, vq = col("pt", gi, 0, 4 * n), sem["vq%d" % gi]
        if gi == 0:
            V.wait_ge(sem.fl, 1)
        V.wait_ge(sem["ex%d" % gi], 4)
        V.tensor_scalar(p, p, T.flo[:, 0:1], None, MAX).then_inc(vq, 1)
        V.wait_ge(vq, 1)
        V.quantize_mx(col("pc", gi, 0, n), col("pp", gi, 0, n), p).then_inc(vq, 1)

    def sums_out(gi):
        n = nn[gi]
        V.wait_ge(sem["pL%d" % gi], 1)
        V.transpose(col("lt", gi, 0, n), ps(gi, 3, n)).then_inc(sem["lt%d" % gi], 1)
        V.wait_ge(sem["lt%d" % gi], 1)
        for k in range(len(G[gi])):
            buf, o = message(gi, k)
            V.tensor_copy(buf[:, o + 128:o + 132], col("lt", gi, 128 * k, 128 * k + 128, 32)).then_inc(sem["lt%d" % gi], 1)

    def products_out(gi):
        S.wait_ge(sem["pA%d" % gi], 1)
        c0 = 512 * (4 * (gi % 2) + 2)
        for k in range(len(G[gi])):
            buf, o = message(gi, k)
            S.activation(buf[:, o:o + 128], T.ps[:, c0 + 128 * k:c0 + 128 * k + 128], Act.Copy).then_inc(sem["ae%d" % gi], 1)

    def send(gi, lo, hi, name):
        tr = []
        for k, (d, es) in enumerate(zip(G[gi], split(me, G[gi]))):
            o, h = (2 * gi + k) * W1, me * W1
            tr.append(RemoteDMATransfer(dst_ids=[dst(d)], dma_engine_mask=to_mask(es), remote_sem=sem["%s%d" % (name, me)],
                                        src=T.out[:, o + lo:o + hi], dst=T.la[:, h + lo:h + hi]))
            sent[0] += len(es)
        fused(tr)

    def send_c(gi):
        g.wait_ge(sem["cc%d" % gi], len(G[gi]))
        if not early(me, gi):
            send(gi, 132, 136, "cm")

    def send_al(gi):
        g.wait_ge(sem["lt%d" % gi], 1 + len(G[gi]))
        if not early(me, gi):
            send(gi, 128, 132, "lm")
        g.wait_ge(sem["ae%d" % gi], len(G[gi]))
        send(gi, 0, W1 if early(me, gi) else 128, "am")

    scores(0)
    for gi in range(NG):
        if gi + 1 < NG:
            scores(gi + 1)
        products(gi)

    maxima(0)
    for gi in range(NG):
        if gi == 0 or not inter[gi - 1]:
            if gi > 0:
                maxima(gi)
            fold(gi)
            if gi > 0:
                sums_out(gi - 1)
            spread(gi)
        subtract(gi)
        if gi == 0:
            V.wait_ge(sem.ldv, 16)
            V.quantize_mx(T.Vc[:], T.Vp[:], T.vb[:]).then_inc(sem.zv, 1)
        if inter[gi]:
            maxima(gi + 1)
        pack(gi)
        if inter[gi]:
            fold(gi + 1)
            sums_out(gi)
            spread(gi + 1)
    sums_out(NG - 1)

    first_copy(0)
    for gi in range(NG):
        shifts_out(gi)
        shift_rows(gi)
        if inter[gi]:
            first_copy(gi + 1)
        exps(gi)
        if gi + 1 < NG and not inter[gi]:
            first_copy(gi + 1)
        products_out(gi)

    for gi in range(1, NG):
        send_c(gi)
        send_al(gi)
    g.sem_inc(sem.go, 1)

    def arrive(j, what):
        gj = group_of(j, me)
        c = len(split(j, groups(j)[gj])[groups(j)[gj].index(me)])
        return sem["%s%d" % ("am" if early(j, gj) else what, j)], c

    rest = [j for j in range(N) if j != me]
    rest.sort(key=lambda j: (group_of(j, me) + (0 if near(j, me) else 0.5), j))
    V.wait_ge(sem.cc0, 1)
    for j in rest:
        V.wait_ge(*arrive(j, "cm"))
    for B in range(4):
        V.tensor_reduce(T.negm[:, B:B + 1], T.la[:, 132 + B:N * W1:W1], AxisListType.X, MAX, negate=True).then_inc(sem.hm, 1)
    S.wait_ge(sem.hm, 4)
    S.wait_ge(sem.ms, 3)
    for B in range(4):
        S.activation(T.wx[:, 32 * B:768:128], T.la[:, 132 + B:N * W1:W1], Act.Exp, bias=T.negm[:, B:B + 1]).then_inc(sem.hx, 1)
    hv = [0]

    def inc(call):
        call.then_inc(sem.hv, 1)
        hv[0] += 1

    def done():
        V.wait_ge(sem.hv, hv[0])

    V.wait_ge(sem.hx, 4)
    inc(V.tensor_tensor_scan(T.ws[:], T.rst[:], T.wx[:], 0.0, ADD, MAX))
    done()
    V.transpose(T.wt[:], T.ws[:]).then_inc(sem.hr, 1)
    V.wait_ge(sem.hr, 1)

    def weigh(out, j, w):
        inc(V.tensor_tensor(out, T.la[:, W1 * j:W1 * j + 128], w, MUL))

    def wt(j):
        return T.wt[:, 128 * j:128 * j + 128]

    V.wait_ge(sem.ae0, 1)
    weigh(T.acc[:], me, wt(me))
    for i, j in enumerate(rest[:-1]):
        V.wait_ge(*arrive(j, "am"))
        weigh(T.tmp[:, 128 * i:128 * i + 128], j, wt(j))
        done()
        inc(V.tensor_tensor(T.acc[:], T.acc[:], T.tmp[:, 128 * i:128 * i + 128], ADD))
    V.wait_ge(sem.lt0, 2)
    for j in rest:
        V.wait_ge(*arrive(j, "lm"))
    for B in range(4):
        inc(V.tensor_tensor(T.wl[:, 6 * B:6 * B + 6], T.la[:, 128 + B:N * W1:W1], T.wx[:, 32 * B:768:128], MUL))
    done()
    for B in range(4):
        inc(V.tensor_reduce(T.den[:, B:B + 1], T.wl[:, 6 * B:6 * B + 6], AxisListType.X, ADD))
    done()
    inc(V.reciprocal(T.rx[:, 0:128:32], T.den[:]))
    done()
    inc(V.tensor_tensor_scan(T.rs[:], T.rst[:, 0:128], T.rx[:], 0.0, ADD, MAX))
    done()
    inc(V.transpose(T.rd[:], T.rs[:]))
    done()
    inc(V.tensor_tensor(T.acc[:], T.acc[:], T.rd[:], MUL))
    j = rest[-1]
    inc(V.tensor_tensor(T.fl[:], wt(j), T.rd[:], MUL))
    done()
    V.wait_ge(*arrive(j, "am"))
    weigh(T.tmp[:, 640:768], j, T.fl[:])
    done()
    V.tensor_tensor(T.osb[:], T.acc[:], T.tmp[:, 640:768], ADD).then_inc(sem.ha, 1)

    stores = [0]

    def store(out, in_):
        Y.dma_start(out, in_).then_inc(sem.st, 16)
        stores[0] += 16

    for gi in range(NG):
        Y.wait_ge(sem["vq%d" % gi], 1)
        if gi == NG - 1:
            Y.wait_ge(sem.go, 1)
        for k, d in enumerate(G[gi]):
            store(T.p[d], col("pt", gi, 512 * k, 512 * k + 512))
    for gi in range(NG):
        Y.wait_ge(sem["cr%d" % gi], len(G[gi]))
    store(T.c[:], T.crow[0:1, :])
    Y.wait_ge(sem.hr, 1)
    store(T.w[:], T.wt[0:1, :])
    Y.wait_ge(sem.ha, 1)
    store(T.o[:], T.osb[:])
    Y.wait_ge(sem.st, stores[0])
    g.wait_ge(sem.sent, sent[0])
